import numpy as np
import ml_dtypes


def mxq(x, axis, fmt="e4m3"):
    dtype, down = {"e4m3": (ml_dtypes.float8_e4m3fn, 7), "e5m2": (ml_dtypes.float8_e5m2, 14)}[fmt]
    v = np.moveaxis(np.asarray(x, np.float32).astype(ml_dtypes.bfloat16).astype(np.float64), axis, -1)
    blocks = v.reshape(v.shape[:-1] + (-1, 32))
    amax = np.abs(blocks).max(-1, keepdims=True)
    byte = np.maximum(np.where(amax > 0, np.frexp(amax)[1] - 1 + 127, 0) - down, 1)
    scale = np.exp2(byte - 127.0)
    codes = (blocks / scale).astype(np.float32).astype(dtype).astype(np.float64)
    return np.moveaxis((codes * scale).reshape(v.shape), -1, axis)


WIDE = False


def mx_kscale(k):
    if not WIDE:
        return np.ones(k)
    levels = np.array([10, -10, 5, -5, 0])
    if k % 512:
        return np.exp2(np.random.permutation(np.resize(levels, k // 32))).repeat(32)
    a = np.empty((k // 512, 16))
    for p in range(k // 512):
        a[p, :8] = np.random.permutation(np.resize(levels, 8))
        for g in range(8):
            far = levels[np.abs(levels - a[p, g]) >= 10]
            a[p, g + 8] = far[np.random.randint(len(far))]
    return np.exp2(a.ravel()).repeat(32)


def f64(x):
    return np.asarray(x).astype(np.float64)


E2M1 = np.array([0.0, 0.5, 1.0, 1.5, 2.0, 3.0, 4.0, 6.0, -0.0, -0.5, -1.0, -1.5, -2.0, -3.0, -4.0, -6.0])


def pack_weight(w, fmt):
    k, n = w.shape
    w = f64(np.asarray(w, np.float32).astype(ml_dtypes.bfloat16)).reshape(k // 32, 32, n)
    amax = np.abs(w).max(1)
    if fmt == "e4m3":
        byte = np.frexp(amax)[1] - 1 + 127 - 7
    else:
        mant, ex = np.frexp(amax / 6.0)
        byte = np.where(mant > 0.5, ex, ex - 1) + 127
    byte = np.clip(np.where(amax > 0, byte, 1), 1, 254)
    scaled = (w * np.exp2(127.0 - byte)[:, None, :]).reshape(k, n).astype(np.float32)
    by_word = np.ascontiguousarray(scaled.reshape(k // 512, 128, 4, n).transpose(0, 1, 3, 2))
    if fmt == "e4m3":
        words = by_word.astype(ml_dtypes.float8_e4m3fn).view(np.uint8)
    else:
        c = by_word.astype(ml_dtypes.float4_e2m1fn).view(np.uint8) & 0xF
        words = (c[..., 0::2] | (c[..., 1::2] << 4)).reshape(k // 512, 128, 2 * n)
    return np.ascontiguousarray(words), np.ascontiguousarray(byte.astype(np.uint8).reshape(k // 512, 16, n))


def unpack_weight(words, scales, fmt):
    g, _, n = scales.shape
    words = np.ascontiguousarray(words).reshape(g, 128, n, -1)
    if fmt == "e4m3":
        vals = words.view(ml_dtypes.float8_e4m3fn).astype(np.float64)
    else:
        nib = np.empty((g, 128, n, 4), np.uint8)
        nib[..., 0::2] = words & 0xF
        nib[..., 1::2] = words >> 4
        vals = E2M1[nib]
    vals = vals * np.repeat(np.exp2(scales.astype(np.float64) - 127.0), 8, axis=1)[..., None]
    return vals.transpose(0, 1, 3, 2).reshape(g * 512, n)


def planes(y):
    n, m = y.shape
    v = y.astype(np.float32).astype(ml_dtypes.bfloat16).astype(np.float64).reshape(n // 32, 32, m)
    top = np.abs(v).max(1)
    byte = np.clip(np.where(top > 0, np.frexp(top)[1] - 1 + 127 - 7, 1), 1, 254)
    codes = (v * np.exp2(127.0 - byte)[:, None, :]).reshape(n, m).astype(np.float32).astype(ml_dtypes.float8_e4m3fn).view(np.uint8)
    words = codes.reshape(n // 512, 128, 4, m).transpose(0, 1, 3, 2)
    return np.ascontiguousarray(words), np.ascontiguousarray(byte.astype(np.uint8).reshape(n // 512, 16, m))


K, M, T = 1024, 1536, 512


def setup_inputs():
    n = np.random.standard_normal
    s = mx_kscale(K)[:, None]
    x = n((K, T)) * s
    x4 = pack_weight(x, "e2m1")
    rest = x - unpack_weight(*x4, "e2m1")
    p_w4 = pack_weight(n((K, M)) / np.sqrt(K) / s, "e2m1")
    return {
        "x4_words": x4[0],
        "x4_scales": x4[1],
        "xr": (rest).astype(np.float32),
        "w4_words": p_w4[0],
        "w4_scales": p_w4[1],
        "r": (n((1536, 512))).astype(np.float32),
    }


def reference(x4_words, x4_scales, xr, w4_words, w4_scales, r):
    x4_ = unpack_weight(x4_words, x4_scales, "e2m1")
    xr_ = mxq(f64(xr), 0, "e4m3")
    w4_ = unpack_weight(w4_words, w4_scales, "e2m1")
    y = w4_.T @ x4_ + w4_.T @ xr_
    out_0 = f64(r) + y
    return (out_0,) + planes(out_0)

@@ -1,0 +1,194 @@
+from contextlib import ExitStack
+
+import concourse.mybir as mybir
+
+K, M, T = 1024, 1536, 512
+FLOPS = 2 * 2 * K * M * T
+
+F32 = mybir.dt.float32
+BF16 = mybir.dt.bfloat16
+I32 = mybir.dt.int32
+U32 = mybir.dt.uint32
+U8 = mybir.dt.uint8
+FP8X4 = mybir.dt.float8_e4m3fn_x4
+FP4X4 = mybir.dt.float4_e2m1fn_x4
+ADD = mybir.AluOpType.add
+
+P = 128
+PACK = 4
+SPAN = P * PACK
+PASSES = K // SPAN
+BLOCKS = M // SPAN
+BANKS = 8
+TAIL_SCALAR_COLS = 160
+XR_VECTOR_COLS = 320
+
+
+def interleave(copy, dst, src, cols):
+    copy(
+        out=dst[:, cols, :].rearrange("p (c i) j -> p c j i", i=PACK),
+        in_=src[:, :, cols].rearrange("p j (c i) -> p c j i", i=PACK),
+    )
+
+
+def tile_mix_xres_fm_pl_res_kernel(
+    tc, x4_words, x4_scales, xr, w4_words, w4_scales, r, out_0, out_1, out_2
+):
+    nc = tc.nc
+    with ExitStack() as ctx:
+        sb = ctx.enter_context(tc.tile_pool(name="sb", bufs=1))
+        psum = ctx.enter_context(tc.psum_pool(name="psum", bufs=1))
+        ctx.enter_context(tc.manual_schedule())
+
+        def tile(name, shape, dtype):
+            return sb.tile(shape, dtype, name=name, align_bytes=256)
+
+        w_first = tile("w_first", [P, PASSES, 2 * SPAN], U8)
+        w_rest = tile("w_rest", [P, PASSES, 2 * (M - SPAN)], U8)
+        ws_raw = tile("ws_raw", [P, PASSES, M], U8)
+        w_dealt = [tile("w_dealt%d" % a, [P, PACK, PASSES, 2 * P], U8) for a in range(BLOCKS)]
+        ws_dealt = [tile("ws_dealt%d" % a, [P, PACK, PASSES, P], U8) for a in range(BLOCKS)]
+        x4_sb = tile("x4_sb", [P, PASSES, 2 * T], U8)
+        x4s_sb = tile("x4s_sb", [P, PASSES, T], U8)
+        xr_f32 = [tile("xr_f32_%d" % g, [P, PACK, T], F32) for g in range(PASSES)]
+        xr_bf = [tile("xr_bf%d" % g, [P, T, PACK], BF16) for g in range(PASSES)]
+        xr_codes = [tile("xr_codes%d" % g, [P, T], U32) for g in range(PASSES)]
+        xr_scales = [tile("xr_scales%d" % g, [P, T], U8) for g in range(PASSES)]
+        r_sb = [tile("r_sb%d" % a, [P, PACK, T], F32) for a in range(BLOCKS)]
+        o_f32 = [tile("o_f32_%d" % a, [P, PACK, T], F32) for a in range(BLOCKS)]
+        o_bf = [tile("o_bf%d" % a, [P, T, PACK], BF16) for a in range(BLOCKS)]
+        o_codes = [tile("o_codes%d" % a, [P, T], U32) for a in range(BLOCKS)]
+        o_scales = tile("o_scales", [P, BLOCKS, T], U8)
+
+        w_hbm = w4_words.bitcast(I32).rearrange("g p n -> p g n")
+        first_words = 2 * SPAN // 4
+
+        def load_scale_rows(queue, plane, scales):
+            rows = scales.bitcast(I32).rearrange("g (q i) n -> i q g n", i=4)
+            for i in range(4):
+                queue.dma_start(out=plane[i:P:32].bitcast(I32), in_=rows[i])
+
+        def rows_of(hbm, a):
+            return hbm[a * SPAN : (a + 1) * SPAN, :].rearrange("(p j) t -> p j t", j=PACK)
+
+        nc.vector.memset(ws_raw[:].bitcast(I32), 0)
+        nc.gpsimd.memset(x4s_sb[:].bitcast(I32), 0)
+
+        nc.sync.dma_start(out=w_first[:].bitcast(I32), in_=w_hbm[:, :, :first_words])
+        load_scale_rows(nc.sync, ws_raw, w4_scales)
+        nc.sync.dma_start(
+            out=x4_sb[:].bitcast(I32), in_=x4_words.bitcast(I32).rearrange("g p n -> p g n")
+        )
+        nc.sync.dma_start(out=w_rest[:].bitcast(I32), in_=w_hbm[:, :, first_words:])
+        load_scale_rows(nc.sync, x4s_sb, x4_scales)
+        nc.sync.dma_start(out=xr_f32[0][:], in_=rows_of(xr, 0))
+        nc.sync.dma_start(out=xr_f32[1][:], in_=rows_of(xr, 1))
+        nc.sync.dma_start(out=r_sb[0][:, 0:2], in_=rows_of(r, 0)[:, 0:2])
+        nc.sync.dma_start(out=r_sb[0][:, 2:4], in_=rows_of(r, 0)[:, 2:4])
+        for a in range(1, BLOCKS):
+            nc.sync.dma_start(out=r_sb[a][:], in_=rows_of(r, a))
+
+        def deal_words(a):
+            raw = w_first[:] if a == 0 else w_rest[:, :, (a - 1) * 2 * SPAN : a * 2 * SPAN]
+            nc.vector.tensor_copy(
+                out=w_dealt[a][:].rearrange("p j g (m b) -> p j g m b", b=2),
+                in_=raw.rearrange("p g (m j b) -> p j g m b", j=PACK, b=2),
+            )
+
+        def deal_scales(a, js):
+            raw = ws_raw[:, :, a * SPAN : (a + 1) * SPAN]
+            nc.vector.tensor_copy(
+                out=ws_dealt[a][:, js], in_=raw.rearrange("p g (m j) -> p j g m", j=PACK)[:, js]
+            )
+
+        def quantize(codes, scales, values):
+            nc.vector.quantize_mx(
+                out=codes.bitcast(FP8X4), scales=scales, in_=values.rearrange("p t j -> p (t j)")
+            )
+
+        acc = {}
+
+        def mm(a, j, g, tier):
+            first = tier == "x4" and g == 0
+            if first:
+                acc[a, j] = psum.tile([P, T], F32, name="bank%d" % ((a * PACK + j) % BANKS))
+            if tier == "x4":
+                rhs, rhs_scale = x4_sb[:, g, :].bitcast(FP4X4), x4s_sb[:, g, :]
+            else:
+                rhs, rhs_scale = xr_codes[g][:].bitcast(FP8X4), xr_scales[g][:]
+            nc.tensor.matmul_mx(
+                out=acc[a, j][:],
+                lhsT=w_dealt[a][:, j, g, :].bitcast(FP4X4),
+                lhsT_scale=ws_dealt[a][:, j, g, :],
+                rhs=rhs,
+                rhs_scale=rhs_scale,
+                start=first,
+                stop=(tier == "xr" and g == PASSES - 1),
+            )
+
+        def add(a, j):
+            nc.vector.tensor_tensor(out=o_f32[a][:, j, :], in0=acc[a, j][:], in1=r_sb[a][:, j, :], op=ADD)
+
+        def store_rows(a, js):
+            nc.sync.dma_start(out=rows_of(out_0, a)[:, js], in_=o_f32[a][:, js])
+
+        def quantize_out(a):
+            quantize(o_codes[a][:], o_scales[:, a, :], o_bf[a][:])
+            nc.sync.dma_start(
+                out=out_1[a].rearrange("p t i -> p (t i)").bitcast(I32), in_=o_codes[a][:].bitcast(I32)
+            )
+
+        def store_scales(queue, blocks):
+            rows = out_2.bitcast(I32).rearrange("a q n -> q a n")
+            for q in range(4):
+                queue.dma_start(
+                    out=rows[4 * q : 4 * q + 4, blocks],
+                    in_=o_scales[32 * q : 32 * q + 4, blocks].bitcast(I32),
+                )
+
+        deal_words(0)
+        deal_scales(0, slice(0, 2))
+        deal_scales(0, slice(2, 4))
+        for a in range(1, BLOCKS):
+            deal_words(a)
+            deal_scales(a, slice(0, PACK))
+        for a in range(2):
+            for j in range(PACK):
+                for g in range(PASSES):
+                    mm(a, j, g, "x4")
+
+        interleave(nc.scalar.copy, xr_bf[0], xr_f32[0], slice(0, T))
+        interleave(nc.vector.tensor_copy, xr_bf[1], xr_f32[1], slice(0, XR_VECTOR_COLS))
+        interleave(nc.scalar.copy, xr_bf[1], xr_f32[1], slice(XR_VECTOR_COLS, T))
+        for g in range(PASSES):
+            quantize(xr_codes[g][:], xr_scales[g][:], xr_bf[g][:])
+
+        for j in range(PACK):
+            mm(0, j, 0, "xr")
+        for j in range(PACK):
+            mm(0, j, 1, "xr")
+            add(0, j)
+            if j % 2:
+                store_rows(0, slice(j - 1, j + 1))
+        interleave(nc.scalar.copy, o_bf[0], o_f32[0], slice(0, T))
+        for j in range(PACK):
+            mm(1, j, 0, "xr")
+            mm(1, j, 1, "xr")
+            add(1, j)
+            if j % 2:
+                store_rows(1, slice(j - 1, j + 1))
+        interleave(nc.scalar.copy, o_bf[1], o_f32[1], slice(0, T))
+        quantize_out(0)
+        for j in range(PACK):
+            for tier in ("x4", "xr"):
+                for g in range(PASSES):
+                    mm(2, j, g, tier)
+            add(2, j)
+            store_rows(2, slice(j, j + 1))
+            if j == 2:
+                quantize_out(1)
+                store_scales(nc.sync, slice(0, 2))
+        interleave(nc.scalar.copy, o_bf[2], o_f32[2], slice(0, TAIL_SCALAR_COLS))
+        interleave(nc.vector.tensor_copy, o_bf[2], o_f32[2], slice(TAIL_SCALAR_COLS, T))
+        quantize_out(2)
+        store_scales(nc.scalar, slice(2, 3))

@@ -21,7 +21,8 @@ PASSES = K // SPAN
 BLOCKS = M // SPAN
 BANKS = 8
 TAIL_SCALAR_COLS = 160
-XR_VECTOR_COLS = 320
+XR_SCALAR_COLS = (288, 160)
+MID_SCALAR_COLS = 384
 
 
 def interleave(copy, dst, src, cols):
@@ -58,7 +59,8 @@ def tile_mix_xres_fm_pl_res_kernel(
         o_f32 = [tile("o_f32_%d" % a, [P, PACK, T], F32) for a in range(BLOCKS)]
         o_bf = [tile("o_bf%d" % a, [P, T, PACK], BF16) for a in range(BLOCKS)]
         o_codes = [tile("o_codes%d" % a, [P, T], U32) for a in range(BLOCKS)]
-        o_scales = tile("o_scales", [P, BLOCKS, T], U8)
+        o_scales_early = tile("o_scales_early", [P, BLOCKS - 1, T], U8)
+        o_scales_last = tile("o_scales_last", [P, 1, T], U8)
 
         w_hbm = w4_words.bitcast(I32).rearrange("g p n -> p g n")
         first_words = 2 * SPAN // 4
@@ -71,8 +73,9 @@ def tile_mix_xres_fm_pl_res_kernel(
         def rows_of(hbm, a):
             return hbm[a * SPAN : (a + 1) * SPAN, :].rearrange("(p j) t -> p j t", j=PACK)
 
-        nc.vector.memset(ws_raw[:].bitcast(I32), 0)
-        nc.gpsimd.memset(x4s_sb[:].bitcast(I32), 0)
+        nc.vector.memset(ws_raw[:, 0, :].bitcast(I32), 0)
+        nc.gpsimd.memset(ws_raw[:, 1, :].bitcast(I32), 0)
+        nc.vector.memset(x4s_sb[:].bitcast(I32), 0)
 
         nc.sync.dma_start(out=w_first[:].bitcast(I32), in_=w_hbm[:, :, :first_words])
         load_scale_rows(nc.sync, ws_raw, w4_scales)
@@ -133,18 +136,16 @@ def tile_mix_xres_fm_pl_res_kernel(
             nc.sync.dma_start(out=rows_of(out_0, a)[:, js], in_=o_f32[a][:, js])
 
         def quantize_out(a):
-            quantize(o_codes[a][:], o_scales[:, a, :], o_bf[a][:])
+            plane = o_scales_last[:, 0, :] if a == BLOCKS - 1 else o_scales_early[:, a, :]
+            quantize(o_codes[a][:], plane, o_bf[a][:])
             nc.sync.dma_start(
                 out=out_1[a].rearrange("p t i -> p (t i)").bitcast(I32), in_=o_codes[a][:].bitcast(I32)
             )
 
-        def store_scales(queue, blocks):
-            rows = out_2.bitcast(I32).rearrange("a q n -> q a n")
-            for q in range(4):
-                queue.dma_start(
-                    out=rows[4 * q : 4 * q + 4, blocks],
-                    in_=o_scales[32 * q : 32 * q + 4, blocks].bitcast(I32),
-                )
+        def store_scales(queue, planes, blocks):
+            rows = out_2.bitcast(I32).rearrange("a (q i) n -> i q a n", i=4)
+            for i in range(4):
+                queue.dma_start(out=rows[i][:, blocks], in_=planes[i:P:32].bitcast(I32))
 
         deal_words(0)
         deal_scales(0, slice(0, 2))
@@ -157,10 +158,9 @@ def tile_mix_xres_fm_pl_res_kernel(
                 for g in range(PASSES):
                     mm(a, j, g, "x4")
 
-        interleave(nc.scalar.copy, xr_bf[0], xr_f32[0], slice(0, T))
-        interleave(nc.vector.tensor_copy, xr_bf[1], xr_f32[1], slice(0, XR_VECTOR_COLS))
-        interleave(nc.scalar.copy, xr_bf[1], xr_f32[1], slice(XR_VECTOR_COLS, T))
         for g in range(PASSES):
+            interleave(nc.scalar.copy, xr_bf[g], xr_f32[g], slice(0, XR_SCALAR_COLS[g]))
+            interleave(nc.vector.tensor_copy, xr_bf[g], xr_f32[g], slice(XR_SCALAR_COLS[g], T))
             quantize(xr_codes[g][:], xr_scales[g][:], xr_bf[g][:])
 
         for j in range(PACK):
@@ -177,18 +177,21 @@ def tile_mix_xres_fm_pl_res_kernel(
             add(1, j)
             if j % 2:
                 store_rows(1, slice(j - 1, j + 1))
-        interleave(nc.scalar.copy, o_bf[1], o_f32[1], slice(0, T))
-        quantize_out(0)
+        interleave(nc.scalar.copy, o_bf[1], o_f32[1], slice(0, MID_SCALAR_COLS))
         for j in range(PACK):
             for tier in ("x4", "xr"):
                 for g in range(PASSES):
                     mm(2, j, g, tier)
             add(2, j)
             store_rows(2, slice(j, j + 1))
+            if j == 0:
+                quantize_out(0)
+            if j == 1:
+                interleave(nc.vector.tensor_copy, o_bf[1], o_f32[1], slice(MID_SCALAR_COLS, T))
             if j == 2:
                 quantize_out(1)
-                store_scales(nc.sync, slice(0, 2))
+                store_scales(nc.sync, o_scales_early, slice(0, 2))
         interleave(nc.scalar.copy, o_bf[2], o_f32[2], slice(0, TAIL_SCALAR_COLS))
         interleave(nc.vector.tensor_copy, o_bf[2], o_f32[2], slice(TAIL_SCALAR_COLS, T))
         quantize_out(2)
-        store_scales(nc.scalar, slice(2, 3))
+        store_scales(nc.scalar, o_scales_last, slice(2, 3))

@@ -20,9 +20,10 @@ SPAN = P * PACK
 PASSES = K // SPAN
 BLOCKS = M // SPAN
 BANKS = 8
-TAIL_SCALAR_COLS = 160
-XR_SCALAR_COLS = (288, 160)
-MID_SCALAR_COLS = 384
+WARM_PASSES = 4
+EARLY_GROUPS = 1
+TAIL_SCALAR_COLS = 192
+XR_SCALAR_COLS = (288, 192)
 
 
 def interleave(copy, dst, src, cols):
@@ -59,8 +60,7 @@ def tile_mix_xres_fm_pl_res_kernel(
         o_f32 = [tile("o_f32_%d" % a, [P, PACK, T], F32) for a in range(BLOCKS)]
         o_bf = [tile("o_bf%d" % a, [P, T, PACK], BF16) for a in range(BLOCKS)]
         o_codes = [tile("o_codes%d" % a, [P, T], U32) for a in range(BLOCKS)]
-        o_scales_early = tile("o_scales_early", [P, BLOCKS - 1, T], U8)
-        o_scales_last = tile("o_scales_last", [P, 1, T], U8)
+        o_scales = tile("o_scales", [P, BLOCKS, T], U8)
 
         w_hbm = w4_words.bitcast(I32).rearrange("g p n -> p g n")
         first_words = 2 * SPAN // 4
@@ -86,9 +86,7 @@ def tile_mix_xres_fm_pl_res_kernel(
         load_scale_rows(nc.sync, x4s_sb, x4_scales)
         nc.sync.dma_start(out=xr_f32[0][:], in_=rows_of(xr, 0))
         nc.sync.dma_start(out=xr_f32[1][:], in_=rows_of(xr, 1))
-        nc.sync.dma_start(out=r_sb[0][:, 0:2], in_=rows_of(r, 0)[:, 0:2])
-        nc.sync.dma_start(out=r_sb[0][:, 2:4], in_=rows_of(r, 0)[:, 2:4])
-        for a in range(1, BLOCKS):
+        for a in range(BLOCKS):
             nc.sync.dma_start(out=r_sb[a][:], in_=rows_of(r, a))
 
         def deal_words(a):
@@ -136,23 +134,34 @@ def tile_mix_xres_fm_pl_res_kernel(
             nc.sync.dma_start(out=rows_of(out_0, a)[:, js], in_=o_f32[a][:, js])
 
         def quantize_out(a):
-            plane = o_scales_last[:, 0, :] if a == BLOCKS - 1 else o_scales_early[:, a, :]
-            quantize(o_codes[a][:], plane, o_bf[a][:])
+            quantize(o_codes[a][:], o_scales[:, a, :], o_bf[a][:])
             nc.sync.dma_start(
                 out=out_1[a].rearrange("p t i -> p (t i)").bitcast(I32), in_=o_codes[a][:].bitcast(I32)
             )
 
-        def store_scales(queue, planes, blocks):
+        def store_scales():
             rows = out_2.bitcast(I32).rearrange("a (q i) n -> i q a n", i=4)
             for i in range(4):
-                queue.dma_start(out=rows[i][:, blocks], in_=planes[i:P:32].bitcast(I32))
+                nc.sync.dma_start(out=rows[i], in_=o_scales[i:P:32].bitcast(I32))
+
+        warm = psum.tile([P, T], F32, name="bank%d" % (BANKS - 1))
+        for step in range(WARM_PASSES):
+            nc.tensor.matmul_mx(
+                out=warm[:],
+                lhsT=w_first[:, 0, : 2 * P].bitcast(FP4X4),
+                lhsT_scale=ws_raw[:, 0, :P],
+                rhs=w_first[:, 0, :].bitcast(FP4X4),
+                rhs_scale=ws_raw[:, 0, :SPAN],
+                start=True,
+                stop=True,
+            )
 
         deal_words(0)
         deal_scales(0, slice(0, 2))
         deal_scales(0, slice(2, 4))
-        for a in range(1, BLOCKS):
-            deal_words(a)
-            deal_scales(a, slice(0, PACK))
+        deal_words(1)
+        deal_scales(1, slice(0, PACK))
+        deal_words(2)
         for a in range(2):
             for j in range(PACK):
                 for g in range(PASSES):
@@ -162,9 +171,12 @@ def tile_mix_xres_fm_pl_res_kernel(
             interleave(nc.scalar.copy, xr_bf[g], xr_f32[g], slice(0, XR_SCALAR_COLS[g]))
             interleave(nc.vector.tensor_copy, xr_bf[g], xr_f32[g], slice(XR_SCALAR_COLS[g], T))
             quantize(xr_codes[g][:], xr_scales[g][:], xr_bf[g][:])
+        deal_scales(2, slice(0, PACK))
 
         for j in range(PACK):
             mm(0, j, 0, "xr")
+        for j in range(EARLY_GROUPS):
+            mm(1, j, 0, "xr")
         for j in range(PACK):
             mm(0, j, 1, "xr")
             add(0, j)
@@ -172,26 +184,23 @@ def tile_mix_xres_fm_pl_res_kernel(
                 store_rows(0, slice(j - 1, j + 1))
         interleave(nc.scalar.copy, o_bf[0], o_f32[0], slice(0, T))
         for j in range(PACK):
-            mm(1, j, 0, "xr")
+            if j >= EARLY_GROUPS:
+                mm(1, j, 0, "xr")
             mm(1, j, 1, "xr")
             add(1, j)
-            if j % 2:
-                store_rows(1, slice(j - 1, j + 1))
-        interleave(nc.scalar.copy, o_bf[1], o_f32[1], slice(0, MID_SCALAR_COLS))
+        store_rows(1, slice(0, PACK))
+        interleave(nc.scalar.copy, o_bf[1], o_f32[1], slice(0, T))
         for j in range(PACK):
             for tier in ("x4", "xr"):
                 for g in range(PASSES):
                     mm(2, j, g, tier)
             add(2, j)
-            store_rows(2, slice(j, j + 1))
+            if j % 2:
+                store_rows(2, slice(j - 1, j + 1))
             if j == 0:
                 quantize_out(0)
-            if j == 1:
-                interleave(nc.vector.tensor_copy, o_bf[1], o_f32[1], slice(MID_SCALAR_COLS, T))
-            if j == 2:
-                quantize_out(1)
-                store_scales(nc.sync, o_scales_early, slice(0, 2))
+        quantize_out(1)
         interleave(nc.scalar.copy, o_bf[2], o_f32[2], slice(0, TAIL_SCALAR_COLS))
         interleave(nc.vector.tensor_copy, o_bf[2], o_f32[2], slice(TAIL_SCALAR_COLS, T))
         quantize_out(2)
-        store_scales(nc.scalar, o_scales_last, slice(2, 3))
+        store_scales()

@@ -20,9 +20,10 @@ SPAN = P * PACK
 PASSES = K // SPAN
 BLOCKS = M // SPAN
 BANKS = 8
-WARM_PASSES = 4
+WARM_PASSES = 3
 EARLY_GROUPS = 1
 TAIL_SCALAR_COLS = 192
+MID_SCALAR_COLS = 400
 XR_SCALAR_COLS = (288, 192)
 
 
@@ -60,7 +61,8 @@ def tile_mix_xres_fm_pl_res_kernel(
         o_f32 = [tile("o_f32_%d" % a, [P, PACK, T], F32) for a in range(BLOCKS)]
         o_bf = [tile("o_bf%d" % a, [P, T, PACK], BF16) for a in range(BLOCKS)]
         o_codes = [tile("o_codes%d" % a, [P, T], U32) for a in range(BLOCKS)]
-        o_scales = tile("o_scales", [P, BLOCKS, T], U8)
+        o_scales_early = tile("o_scales_early", [P, BLOCKS - 1, T], U8)
+        o_scales_last = tile("o_scales_last", [P, 1, T], U8)
 
         w_hbm = w4_words.bitcast(I32).rearrange("g p n -> p g n")
         first_words = 2 * SPAN // 4
@@ -134,15 +136,16 @@ def tile_mix_xres_fm_pl_res_kernel(
             nc.sync.dma_start(out=rows_of(out_0, a)[:, js], in_=o_f32[a][:, js])
 
         def quantize_out(a):
-            quantize(o_codes[a][:], o_scales[:, a, :], o_bf[a][:])
+            plane = o_scales_last[:, 0, :] if a == BLOCKS - 1 else o_scales_early[:, a, :]
+            quantize(o_codes[a][:], plane, o_bf[a][:])
             nc.sync.dma_start(
                 out=out_1[a].rearrange("p t i -> p (t i)").bitcast(I32), in_=o_codes[a][:].bitcast(I32)
             )
 
-        def store_scales():
+        def store_scales(planes, blocks):
             rows = out_2.bitcast(I32).rearrange("a (q i) n -> i q a n", i=4)
             for i in range(4):
-                nc.sync.dma_start(out=rows[i], in_=o_scales[i:P:32].bitcast(I32))
+                nc.sync.dma_start(out=rows[i][:, blocks], in_=planes[i:P:32].bitcast(I32))
 
         warm = psum.tile([P, T], F32, name="bank%d" % (BANKS - 1))
         for step in range(WARM_PASSES):
@@ -189,7 +192,7 @@ def tile_mix_xres_fm_pl_res_kernel(
             mm(1, j, 1, "xr")
             add(1, j)
         store_rows(1, slice(0, PACK))
-        interleave(nc.scalar.copy, o_bf[1], o_f32[1], slice(0, T))
+        interleave(nc.scalar.copy, o_bf[1], o_f32[1], slice(0, MID_SCALAR_COLS))
         for j in range(PACK):
             for tier in ("x4", "xr"):
                 for g in range(PASSES):
@@ -199,8 +202,11 @@ def tile_mix_xres_fm_pl_res_kernel(
                 store_rows(2, slice(j - 1, j + 1))
             if j == 0:
                 quantize_out(0)
-        quantize_out(1)
+                interleave(nc.vector.tensor_copy, o_bf[1], o_f32[1], slice(MID_SCALAR_COLS, T))
+            if j == 2:
+                quantize_out(1)
+                store_scales(o_scales_early, slice(0, 2))
         interleave(nc.scalar.copy, o_bf[2], o_f32[2], slice(0, TAIL_SCALAR_COLS))
         interleave(nc.vector.tensor_copy, o_bf[2], o_f32[2], slice(TAIL_SCALAR_COLS, T))
         quantize_out(2)
-        store_scales()
+        store_scales(o_scales_last, slice(2, 3))

@@ -9,6 +9,7 @@ F32 = mybir.dt.float32
 BF16 = mybir.dt.bfloat16
 I32 = mybir.dt.int32
 U32 = mybir.dt.uint32
+U16 = mybir.dt.uint16
 U8 = mybir.dt.uint8
 FP8X4 = mybir.dt.float8_e4m3fn_x4
 FP4X4 = mybir.dt.float4_e2m1fn_x4
@@ -20,11 +21,11 @@ SPAN = P * PACK
 PASSES = K // SPAN
 BLOCKS = M // SPAN
 BANKS = 8
-WARM_PASSES = 3
-EARLY_GROUPS = 1
-TAIL_SCALAR_COLS = 192
-MID_SCALAR_COLS = 400
-XR_SCALAR_COLS = (288, 192)
+WARM_PASSES = 4
+EARLY_GROUPS = 2
+OUT_PLANE_ROW = 4
+TAIL_SCALAR_COLS = 256
+XR_SCALAR_COLS = (176, 176)
 
 
 def interleave(copy, dst, src, cols):
@@ -60,9 +61,9 @@ def tile_mix_xres_fm_pl_res_kernel(
         r_sb = [tile("r_sb%d" % a, [P, PACK, T], F32) for a in range(BLOCKS)]
         o_f32 = [tile("o_f32_%d" % a, [P, PACK, T], F32) for a in range(BLOCKS)]
         o_bf = [tile("o_bf%d" % a, [P, T, PACK], BF16) for a in range(BLOCKS)]
-        o_codes = [tile("o_codes%d" % a, [P, T], U32) for a in range(BLOCKS)]
-        o_scales_early = tile("o_scales_early", [P, BLOCKS - 1, T], U8)
-        o_scales_last = tile("o_scales_last", [P, 1, T], U8)
+        o_codes_early = tile("o_codes_early", [P, BLOCKS - 1, T], U32)
+        o_codes_last = tile("o_codes_last", [P, 1, T], U32)
+        o_scales = tile("o_scales", [P, BLOCKS, T], U8)
 
         w_hbm = w4_words.bitcast(I32).rearrange("g p n -> p g n")
         first_words = 2 * SPAN // 4
@@ -75,8 +76,7 @@ def tile_mix_xres_fm_pl_res_kernel(
         def rows_of(hbm, a):
             return hbm[a * SPAN : (a + 1) * SPAN, :].rearrange("(p j) t -> p j t", j=PACK)
 
-        nc.vector.memset(ws_raw[:, 0, :].bitcast(I32), 0)
-        nc.gpsimd.memset(ws_raw[:, 1, :].bitcast(I32), 0)
+        nc.vector.memset(ws_raw[:].bitcast(I32), 0)
         nc.vector.memset(x4s_sb[:].bitcast(I32), 0)
 
         nc.sync.dma_start(out=w_first[:].bitcast(I32), in_=w_hbm[:, :, :first_words])
@@ -94,8 +94,8 @@ def tile_mix_xres_fm_pl_res_kernel(
         def deal_words(a):
             raw = w_first[:] if a == 0 else w_rest[:, :, (a - 1) * 2 * SPAN : a * 2 * SPAN]
             nc.vector.tensor_copy(
-                out=w_dealt[a][:].rearrange("p j g (m b) -> p j g m b", b=2),
-                in_=raw.rearrange("p g (m j b) -> p j g m b", j=PACK, b=2),
+                out=w_dealt[a][:].bitcast(U16),
+                in_=raw.bitcast(U16).rearrange("p g (m j) -> p j g m", j=PACK),
             )
 
         def deal_scales(a, js):
@@ -136,25 +136,27 @@ def tile_mix_xres_fm_pl_res_kernel(
             nc.sync.dma_start(out=rows_of(out_0, a)[:, js], in_=o_f32[a][:, js])
 
         def quantize_out(a):
-            plane = o_scales_last[:, 0, :] if a == BLOCKS - 1 else o_scales_early[:, a, :]
-            quantize(o_codes[a][:], plane, o_bf[a][:])
+            codes = o_codes_last[:, 0, :] if a == BLOCKS - 1 else o_codes_early[:, a, :]
+            quantize(codes, o_scales[OUT_PLANE_ROW:P, a, :], o_bf[a][:])
+
+        def store_codes(codes, blocks):
             nc.sync.dma_start(
-                out=out_1[a].rearrange("p t i -> p (t i)").bitcast(I32), in_=o_codes[a][:].bitcast(I32)
+                out=out_1[blocks].rearrange("a p t i -> p a (t i)").bitcast(I32), in_=codes[:].bitcast(I32)
             )
 
-        def store_scales(planes, blocks):
+        def store_scales():
             rows = out_2.bitcast(I32).rearrange("a (q i) n -> i q a n", i=4)
             for i in range(4):
-                nc.sync.dma_start(out=rows[i][:, blocks], in_=planes[i:P:32].bitcast(I32))
+                nc.sync.dma_start(out=rows[i], in_=o_scales[OUT_PLANE_ROW + i : P : 32].bitcast(I32))
 
         warm = psum.tile([P, T], F32, name="bank%d" % (BANKS - 1))
         for step in range(WARM_PASSES):
             nc.tensor.matmul_mx(
                 out=warm[:],
                 lhsT=w_first[:, 0, : 2 * P].bitcast(FP4X4),
-                lhsT_scale=ws_raw[:, 0, :P],
+                lhsT_scale=w_first[:, 1, :P],
                 rhs=w_first[:, 0, :].bitcast(FP4X4),
-                rhs_scale=ws_raw[:, 0, :SPAN],
+                rhs_scale=w_first[:, 1, :SPAN],
                 start=True,
                 stop=True,
             )
@@ -162,8 +164,9 @@ def tile_mix_xres_fm_pl_res_kernel(
         deal_words(0)
         deal_scales(0, slice(0, 2))
         deal_scales(0, slice(2, 4))
-        deal_words(1)
         deal_scales(1, slice(0, PACK))
+        deal_scales(2, slice(0, PACK))
+        deal_words(1)
         deal_words(2)
         for a in range(2):
             for j in range(PACK):
@@ -174,7 +177,6 @@ def tile_mix_xres_fm_pl_res_kernel(
             interleave(nc.scalar.copy, xr_bf[g], xr_f32[g], slice(0, XR_SCALAR_COLS[g]))
             interleave(nc.vector.tensor_copy, xr_bf[g], xr_f32[g], slice(XR_SCALAR_COLS[g], T))
             quantize(xr_codes[g][:], xr_scales[g][:], xr_bf[g][:])
-        deal_scales(2, slice(0, PACK))
 
         for j in range(PACK):
             mm(0, j, 0, "xr")
@@ -191,8 +193,9 @@ def tile_mix_xres_fm_pl_res_kernel(
                 mm(1, j, 0, "xr")
             mm(1, j, 1, "xr")
             add(1, j)
-        store_rows(1, slice(0, PACK))
-        interleave(nc.scalar.copy, o_bf[1], o_f32[1], slice(0, MID_SCALAR_COLS))
+            if j % 2:
+                store_rows(1, slice(j - 1, j + 1))
+        interleave(nc.scalar.copy, o_bf[1], o_f32[1], slice(0, T))
         for j in range(PACK):
             for tier in ("x4", "xr"):
                 for g in range(PASSES):
@@ -202,11 +205,10 @@ def tile_mix_xres_fm_pl_res_kernel(
                 store_rows(2, slice(j - 1, j + 1))
             if j == 0:
                 quantize_out(0)
-                interleave(nc.vector.tensor_copy, o_bf[1], o_f32[1], slice(MID_SCALAR_COLS, T))
-            if j == 2:
-                quantize_out(1)
-                store_scales(o_scales_early, slice(0, 2))
         interleave(nc.scalar.copy, o_bf[2], o_f32[2], slice(0, TAIL_SCALAR_COLS))
+        quantize_out(1)
+        store_codes(o_codes_early, slice(0, BLOCKS - 1))
         interleave(nc.vector.tensor_copy, o_bf[2], o_f32[2], slice(TAIL_SCALAR_COLS, T))
         quantize_out(2)
-        store_scales(o_scales_last, slice(2, 3))
+        store_codes(o_codes_last, slice(BLOCKS - 1, BLOCKS))
+        store_scales()

@@ -22,10 +22,12 @@ PASSES = K // SPAN
 BLOCKS = M // SPAN
 BANKS = 8
 WARM_PASSES = 4
-EARLY_GROUPS = 2
+EARLY_GROUPS = 1
 OUT_PLANE_ROW = 4
-TAIL_SCALAR_COLS = 256
-XR_SCALAR_COLS = (176, 176)
+HALF = T // 2
+LEFT, RIGHT, WHOLE = slice(0, HALF), slice(HALF, T), slice(0, T)
+TAIL_SCALAR_COLS = 192
+XR_SCALAR_COLS = 176
 
 
 def interleave(copy, dst, src, cols):
@@ -47,8 +49,7 @@ def tile_mix_xres_fm_pl_res_kernel(
         def tile(name, shape, dtype):
             return sb.tile(shape, dtype, name=name, align_bytes=256)
 
-        w_first = tile("w_first", [P, PASSES, 2 * SPAN], U8)
-        w_rest = tile("w_rest", [P, PASSES, 2 * (M - SPAN)], U8)
+        w_raw = [tile("w_raw%d" % a, [P, PASSES, 2 * SPAN], U8) for a in range(BLOCKS)]
         ws_raw = tile("ws_raw", [P, PASSES, M], U8)
         w_dealt = [tile("w_dealt%d" % a, [P, PACK, PASSES, 2 * P], U8) for a in range(BLOCKS)]
         ws_dealt = [tile("ws_dealt%d" % a, [P, PACK, PASSES, P], U8) for a in range(BLOCKS)]
@@ -61,12 +62,16 @@ def tile_mix_xres_fm_pl_res_kernel(
         r_sb = [tile("r_sb%d" % a, [P, PACK, T], F32) for a in range(BLOCKS)]
         o_f32 = [tile("o_f32_%d" % a, [P, PACK, T], F32) for a in range(BLOCKS)]
         o_bf = [tile("o_bf%d" % a, [P, T, PACK], BF16) for a in range(BLOCKS)]
-        o_codes_early = tile("o_codes_early", [P, BLOCKS - 1, T], U32)
-        o_codes_last = tile("o_codes_last", [P, 1, T], U32)
+        o_codes = [tile("o_codes%d" % a, [P, T], U32) for a in range(BLOCKS)]
         o_scales = tile("o_scales", [P, BLOCKS, T], U8)
 
         w_hbm = w4_words.bitcast(I32).rearrange("g p n -> p g n")
-        first_words = 2 * SPAN // 4
+        block_words = 2 * SPAN // 4
+
+        def load_weights(a):
+            nc.sync.dma_start(
+                out=w_raw[a][:].bitcast(I32), in_=w_hbm[:, :, a * block_words : (a + 1) * block_words]
+            )
 
         def load_scale_rows(queue, plane, scales):
             rows = scales.bitcast(I32).rearrange("g (q i) n -> i q g n", i=4)
@@ -79,23 +84,23 @@ def tile_mix_xres_fm_pl_res_kernel(
         nc.vector.memset(ws_raw[:].bitcast(I32), 0)
         nc.vector.memset(x4s_sb[:].bitcast(I32), 0)
 
-        nc.sync.dma_start(out=w_first[:].bitcast(I32), in_=w_hbm[:, :, :first_words])
+        load_weights(0)
         load_scale_rows(nc.sync, ws_raw, w4_scales)
         nc.sync.dma_start(
             out=x4_sb[:].bitcast(I32), in_=x4_words.bitcast(I32).rearrange("g p n -> p g n")
         )
-        nc.sync.dma_start(out=w_rest[:].bitcast(I32), in_=w_hbm[:, :, first_words:])
+        load_weights(1)
         load_scale_rows(nc.sync, x4s_sb, x4_scales)
         nc.sync.dma_start(out=xr_f32[0][:], in_=rows_of(xr, 0))
         nc.sync.dma_start(out=xr_f32[1][:], in_=rows_of(xr, 1))
+        load_weights(2)
         for a in range(BLOCKS):
             nc.sync.dma_start(out=r_sb[a][:], in_=rows_of(r, a))
 
         def deal_words(a):
-            raw = w_first[:] if a == 0 else w_rest[:, :, (a - 1) * 2 * SPAN : a * 2 * SPAN]
             nc.vector.tensor_copy(
                 out=w_dealt[a][:].bitcast(U16),
-                in_=raw.bitcast(U16).rearrange("p g (m j) -> p j g m", j=PACK),
+                in_=w_raw[a][:].bitcast(U16).rearrange("p g (m j) -> p j g m", j=PACK),
             )
 
         def deal_scales(a, js):
@@ -129,19 +134,20 @@ def tile_mix_xres_fm_pl_res_kernel(
                 stop=(tier == "xr" and g == PASSES - 1),
             )
 
-        def add(a, j):
-            nc.vector.tensor_tensor(out=o_f32[a][:, j, :], in0=acc[a, j][:], in1=r_sb[a][:, j, :], op=ADD)
+        def add(a, j, cols):
+            nc.vector.tensor_tensor(
+                out=o_f32[a][:, j, cols], in0=acc[a, j][:, cols], in1=r_sb[a][:, j, cols], op=ADD
+            )
 
         def store_rows(a, js):
             nc.sync.dma_start(out=rows_of(out_0, a)[:, js], in_=o_f32[a][:, js])
 
-        def quantize_out(a):
-            codes = o_codes_last[:, 0, :] if a == BLOCKS - 1 else o_codes_early[:, a, :]
-            quantize(codes, o_scales[OUT_PLANE_ROW:P, a, :], o_bf[a][:])
+        def quantize_out(a, cols):
+            quantize(o_codes[a][:, cols], o_scales[OUT_PLANE_ROW:P, a, cols], o_bf[a][:, cols, :])
 
-        def store_codes(codes, blocks):
+        def store_codes(a):
             nc.sync.dma_start(
-                out=out_1[blocks].rearrange("a p t i -> p a (t i)").bitcast(I32), in_=codes[:].bitcast(I32)
+                out=out_1[a].rearrange("p t i -> p (t i)").bitcast(I32), in_=o_codes[a][:].bitcast(I32)
             )
 
         def store_scales():
@@ -153,10 +159,10 @@ def tile_mix_xres_fm_pl_res_kernel(
         for step in range(WARM_PASSES):
             nc.tensor.matmul_mx(
                 out=warm[:],
-                lhsT=w_first[:, 0, : 2 * P].bitcast(FP4X4),
-                lhsT_scale=w_first[:, 1, :P],
-                rhs=w_first[:, 0, :].bitcast(FP4X4),
-                rhs_scale=w_first[:, 1, :SPAN],
+                lhsT=w_raw[0][:, 0, : 2 * P].bitcast(FP4X4),
+                lhsT_scale=w_raw[0][:, 1, :P],
+                rhs=w_raw[0][:, 0, :].bitcast(FP4X4),
+                rhs_scale=w_raw[0][:, 1, :SPAN],
                 start=True,
                 stop=True,
             )
@@ -167,48 +173,57 @@ def tile_mix_xres_fm_pl_res_kernel(
         deal_scales(1, slice(0, PACK))
         deal_scales(2, slice(0, PACK))
         deal_words(1)
-        deal_words(2)
         for a in range(2):
             for j in range(PACK):
                 for g in range(PASSES):
                     mm(a, j, g, "x4")
 
         for g in range(PASSES):
-            interleave(nc.scalar.copy, xr_bf[g], xr_f32[g], slice(0, XR_SCALAR_COLS[g]))
-            interleave(nc.vector.tensor_copy, xr_bf[g], xr_f32[g], slice(XR_SCALAR_COLS[g], T))
-            quantize(xr_codes[g][:], xr_scales[g][:], xr_bf[g][:])
+            split = HALF + XR_SCALAR_COLS
+            interleave(nc.scalar.copy, xr_bf[g], xr_f32[g], slice(HALF, split))
+            interleave(nc.vector.tensor_copy, xr_bf[g], xr_f32[g], LEFT)
+            interleave(nc.vector.tensor_copy, xr_bf[g], xr_f32[g], slice(split, T))
+            for cols in (LEFT, RIGHT):
+                quantize(xr_codes[g][:, cols], xr_scales[g][:, cols], xr_bf[g][:, cols, :])
+        deal_words(2)
 
         for j in range(PACK):
             mm(0, j, 0, "xr")
         for j in range(EARLY_GROUPS):
             mm(1, j, 0, "xr")
-        for j in range(PACK):
-            mm(0, j, 1, "xr")
-            add(0, j)
-            if j % 2:
-                store_rows(0, slice(j - 1, j + 1))
-        interleave(nc.scalar.copy, o_bf[0], o_f32[0], slice(0, T))
-        for j in range(PACK):
-            if j >= EARLY_GROUPS:
-                mm(1, j, 0, "xr")
-            mm(1, j, 1, "xr")
-            add(1, j)
-            if j % 2:
-                store_rows(1, slice(j - 1, j + 1))
-        interleave(nc.scalar.copy, o_bf[1], o_f32[1], slice(0, T))
+        for a in range(2):
+            for j in range(PACK):
+                if a == 1 and j >= EARLY_GROUPS:
+                    mm(a, j, 0, "xr")
+                mm(a, j, 1, "xr")
+                add(a, j, LEFT)
+            interleave(nc.scalar.copy, o_bf[a], o_f32[a], LEFT)
+            for j in range(PACK):
+                add(a, j, RIGHT)
+                if j % 2:
+                    store_rows(a, slice(j - 1, j + 1))
+            interleave(nc.scalar.copy, o_bf[a], o_f32[a], RIGHT)
+
+        last = BLOCKS - 1
+        quantize_out(0, WHOLE)
+        store_codes(0)
         for j in range(PACK):
             for tier in ("x4", "xr"):
                 for g in range(PASSES):
-                    mm(2, j, g, tier)
-            add(2, j)
-            if j % 2:
-                store_rows(2, slice(j - 1, j + 1))
-            if j == 0:
-                quantize_out(0)
-        interleave(nc.scalar.copy, o_bf[2], o_f32[2], slice(0, TAIL_SCALAR_COLS))
-        quantize_out(1)
-        store_codes(o_codes_early, slice(0, BLOCKS - 1))
-        interleave(nc.vector.tensor_copy, o_bf[2], o_f32[2], slice(TAIL_SCALAR_COLS, T))
-        quantize_out(2)
-        store_codes(o_codes_last, slice(BLOCKS - 1, BLOCKS))
+                    mm(last, j, g, tier)
+            if j < PACK - 1:
+                add(last, j, WHOLE)
+            if j == 1:
+                store_rows(last, slice(0, 2))
+        quantize_out(1, WHOLE)
+        store_codes(1)
+        add(last, PACK - 1, LEFT)
+        interleave(nc.scalar.copy, o_bf[last], o_f32[last], slice(0, TAIL_SCALAR_COLS))
+        add(last, PACK - 1, RIGHT)
+        store_rows(last, slice(2, PACK))
+        interleave(nc.vector.tensor_copy, o_bf[last], o_f32[last], slice(TAIL_SCALAR_COLS, HALF))
+        interleave(nc.vector.tensor_copy, o_bf[last], o_f32[last], RIGHT)
+        quantize_out(last, LEFT)
+        quantize_out(last, RIGHT)
+        store_codes(last)
         store_scales()

@@ -49,7 +49,9 @@ def tile_mix_xres_fm_pl_res_kernel(
         def tile(name, shape, dtype):
             return sb.tile(shape, dtype, name=name, align_bytes=256)
 
-        w_raw = [tile("w_raw%d" % a, [P, PASSES, 2 * SPAN], U8) for a in range(BLOCKS)]
+        last = BLOCKS - 1
+        w_early = tile("w_early", [P, PASSES, last * 2 * SPAN], U8)
+        w_late = tile("w_late", [P, PASSES, 2 * SPAN], U8)
         ws_raw = tile("ws_raw", [P, PASSES, M], U8)
         w_dealt = [tile("w_dealt%d" % a, [P, PACK, PASSES, 2 * P], U8) for a in range(BLOCKS)]
         ws_dealt = [tile("ws_dealt%d" % a, [P, PACK, PASSES, P], U8) for a in range(BLOCKS)]
@@ -62,16 +64,12 @@ def tile_mix_xres_fm_pl_res_kernel(
         r_sb = [tile("r_sb%d" % a, [P, PACK, T], F32) for a in range(BLOCKS)]
         o_f32 = [tile("o_f32_%d" % a, [P, PACK, T], F32) for a in range(BLOCKS)]
         o_bf = [tile("o_bf%d" % a, [P, T, PACK], BF16) for a in range(BLOCKS)]
-        o_codes = [tile("o_codes%d" % a, [P, T], U32) for a in range(BLOCKS)]
+        codes_early = tile("codes_early", [P, last, T], U32)
+        codes_late = tile("codes_late", [P, T], U32)
         o_scales = tile("o_scales", [P, BLOCKS, T], U8)
 
         w_hbm = w4_words.bitcast(I32).rearrange("g p n -> p g n")
-        block_words = 2 * SPAN // 4
-
-        def load_weights(a):
-            nc.sync.dma_start(
-                out=w_raw[a][:].bitcast(I32), in_=w_hbm[:, :, a * block_words : (a + 1) * block_words]
-            )
+        early_words = last * 2 * SPAN // 4
 
         def load_scale_rows(queue, plane, scales):
             rows = scales.bitcast(I32).rearrange("g (q i) n -> i q g n", i=4)
@@ -84,23 +82,23 @@ def tile_mix_xres_fm_pl_res_kernel(
         nc.vector.memset(ws_raw[:].bitcast(I32), 0)
         nc.vector.memset(x4s_sb[:].bitcast(I32), 0)
 
-        load_weights(0)
-        load_scale_rows(nc.sync, ws_raw, w4_scales)
         nc.sync.dma_start(
             out=x4_sb[:].bitcast(I32), in_=x4_words.bitcast(I32).rearrange("g p n -> p g n")
         )
-        load_weights(1)
+        load_scale_rows(nc.sync, ws_raw, w4_scales)
+        nc.sync.dma_start(out=w_early[:].bitcast(I32), in_=w_hbm[:, :, :early_words])
         load_scale_rows(nc.sync, x4s_sb, x4_scales)
         nc.sync.dma_start(out=xr_f32[0][:], in_=rows_of(xr, 0))
         nc.sync.dma_start(out=xr_f32[1][:], in_=rows_of(xr, 1))
-        load_weights(2)
+        nc.sync.dma_start(out=w_late[:].bitcast(I32), in_=w_hbm[:, :, early_words:])
         for a in range(BLOCKS):
             nc.sync.dma_start(out=r_sb[a][:], in_=rows_of(r, a))
 
-        def deal_words(a):
+        def deal_words(a, js):
+            raw = w_late[:] if a == last else w_early[:, :, a * 2 * SPAN : (a + 1) * 2 * SPAN]
             nc.vector.tensor_copy(
-                out=w_dealt[a][:].bitcast(U16),
-                in_=w_raw[a][:].bitcast(U16).rearrange("p g (m j) -> p j g m", j=PACK),
+                out=w_dealt[a][:, js].bitcast(U16),
+                in_=raw.bitcast(U16).rearrange("p g (m j) -> p j g m", j=PACK)[:, js],
             )
 
         def deal_scales(a, js):
@@ -143,12 +141,10 @@ def tile_mix_xres_fm_pl_res_kernel(
             nc.sync.dma_start(out=rows_of(out_0, a)[:, js], in_=o_f32[a][:, js])
 
         def quantize_out(a, cols):
-            quantize(o_codes[a][:, cols], o_scales[OUT_PLANE_ROW:P, a, cols], o_bf[a][:, cols, :])
+            codes = codes_late[:, cols] if a == last else codes_early[:, a, cols]
+            quantize(codes, o_scales[OUT_PLANE_ROW:P, a, cols], o_bf[a][:, cols, :])
 
-        def store_codes(a):
-            nc.sync.dma_start(
-                out=out_1[a].rearrange("p t i -> p (t i)").bitcast(I32), in_=o_codes[a][:].bitcast(I32)
-            )
+        codes_hbm = out_1.rearrange("a p t i -> p a (t i)").bitcast(I32)
 
         def store_scales():
             rows = out_2.bitcast(I32).rearrange("a (q i) n -> i q a n", i=4)
@@ -159,20 +155,21 @@ def tile_mix_xres_fm_pl_res_kernel(
         for step in range(WARM_PASSES):
             nc.tensor.matmul_mx(
                 out=warm[:],
-                lhsT=w_raw[0][:, 0, : 2 * P].bitcast(FP4X4),
-                lhsT_scale=w_raw[0][:, 1, :P],
-                rhs=w_raw[0][:, 0, :].bitcast(FP4X4),
-                rhs_scale=w_raw[0][:, 1, :SPAN],
+                lhsT=x4_sb[:, 0, : 2 * P].bitcast(FP4X4),
+                lhsT_scale=x4_sb[:, 1, :P],
+                rhs=x4_sb[:, 0, :].bitcast(FP4X4),
+                rhs_scale=x4_sb[:, 1, :T],
                 start=True,
                 stop=True,
             )
 
-        deal_words(0)
-        deal_scales(0, slice(0, 2))
-        deal_scales(0, slice(2, 4))
-        deal_scales(1, slice(0, PACK))
-        deal_scales(2, slice(0, PACK))
-        deal_words(1)
+        front, back, every = slice(0, 2), slice(2, PACK), slice(0, PACK)
+        deal_scales(0, every)
+        deal_words(0, front)
+        deal_words(0, back)
+        deal_scales(1, every)
+        deal_words(1, every)
+        deal_scales(2, every)
         for a in range(2):
             for j in range(PACK):
                 for g in range(PASSES):
@@ -185,8 +182,8 @@ def tile_mix_xres_fm_pl_res_kernel(
             interleave(nc.vector.tensor_copy, xr_bf[g], xr_f32[g], slice(split, T))
             for cols in (LEFT, RIGHT):
                 quantize(xr_codes[g][:, cols], xr_scales[g][:, cols], xr_bf[g][:, cols, :])
-        deal_words(2)
 
+        deal_words(last, every)
         for j in range(PACK):
             mm(0, j, 0, "xr")
         for j in range(EARLY_GROUPS):
@@ -204,9 +201,7 @@ def tile_mix_xres_fm_pl_res_kernel(
                     store_rows(a, slice(j - 1, j + 1))
             interleave(nc.scalar.copy, o_bf[a], o_f32[a], RIGHT)
 
-        last = BLOCKS - 1
         quantize_out(0, WHOLE)
-        store_codes(0)
         for j in range(PACK):
             for tier in ("x4", "xr"):
                 for g in range(PASSES):
@@ -216,14 +211,14 @@ def tile_mix_xres_fm_pl_res_kernel(
             if j == 1:
                 store_rows(last, slice(0, 2))
         quantize_out(1, WHOLE)
-        store_codes(1)
+        nc.sync.dma_start(out=codes_hbm[:, :last], in_=codes_early[:].bitcast(I32))
         add(last, PACK - 1, LEFT)
         interleave(nc.scalar.copy, o_bf[last], o_f32[last], slice(0, TAIL_SCALAR_COLS))
         add(last, PACK - 1, RIGHT)
         store_rows(last, slice(2, PACK))
         interleave(nc.vector.tensor_copy, o_bf[last], o_f32[last], slice(TAIL_SCALAR_COLS, HALF))
         interleave(nc.vector.tensor_copy, o_bf[last], o_f32[last], RIGHT)
-        quantize_out(last, LEFT)
-        quantize_out(last, RIGHT)
-        store_codes(last)
+        for cols in (LEFT, RIGHT):
+            quantize_out(last, cols)
+            nc.sync.dma_start(out=codes_hbm[:, last, cols], in_=codes_late[:, cols].bitcast(I32))
         store_scales()

@@ -22,11 +22,12 @@ PASSES = K // SPAN
 BLOCKS = M // SPAN
 BANKS = 8
 WARM_PASSES = 4
-EARLY_GROUPS = 1
 OUT_PLANE_ROW = 4
 HALF = T // 2
 LEFT, RIGHT, WHOLE = slice(0, HALF), slice(HALF, T), slice(0, T)
-TAIL_SCALAR_COLS = 192
+FRONT, BACK, EVERY = slice(0, 2), slice(2, PACK), slice(0, PACK)
+EARLY_GROUPS = 0
+TAIL_VECTOR_COLS = 128
 XR_SCALAR_COLS = 176
 
 
@@ -71,40 +72,28 @@ def tile_mix_xres_fm_pl_res_kernel(
         w_hbm = w4_words.bitcast(I32).rearrange("g p n -> p g n")
         early_words = last * 2 * SPAN // 4
 
-        def load_scale_rows(queue, plane, scales):
+        def load_scale_rows(plane, scales):
             rows = scales.bitcast(I32).rearrange("g (q i) n -> i q g n", i=4)
             for i in range(4):
-                queue.dma_start(out=plane[i:P:32].bitcast(I32), in_=rows[i])
+                nc.sync.dma_start(out=plane[i:P:32].bitcast(I32), in_=rows[i])
 
         def rows_of(hbm, a):
             return hbm[a * SPAN : (a + 1) * SPAN, :].rearrange("(p j) t -> p j t", j=PACK)
 
-        nc.vector.memset(ws_raw[:].bitcast(I32), 0)
-        nc.vector.memset(x4s_sb[:].bitcast(I32), 0)
+        def load_r(a, js):
+            nc.sync.dma_start(out=r_sb[a][:, js], in_=rows_of(r, a)[:, js])
 
-        nc.sync.dma_start(
-            out=x4_sb[:].bitcast(I32), in_=x4_words.bitcast(I32).rearrange("g p n -> p g n")
-        )
-        load_scale_rows(nc.sync, ws_raw, w4_scales)
-        nc.sync.dma_start(out=w_early[:].bitcast(I32), in_=w_hbm[:, :, :early_words])
-        load_scale_rows(nc.sync, x4s_sb, x4_scales)
-        nc.sync.dma_start(out=xr_f32[0][:], in_=rows_of(xr, 0))
-        nc.sync.dma_start(out=xr_f32[1][:], in_=rows_of(xr, 1))
-        nc.sync.dma_start(out=w_late[:].bitcast(I32), in_=w_hbm[:, :, early_words:])
-        for a in range(BLOCKS):
-            nc.sync.dma_start(out=r_sb[a][:], in_=rows_of(r, a))
-
-        def deal_words(a, js):
+        def deal_words(copy, a, js):
             raw = w_late[:] if a == last else w_early[:, :, a * 2 * SPAN : (a + 1) * 2 * SPAN]
-            nc.vector.tensor_copy(
+            copy(
                 out=w_dealt[a][:, js].bitcast(U16),
                 in_=raw.bitcast(U16).rearrange("p g (m j) -> p j g m", j=PACK)[:, js],
             )
 
-        def deal_scales(a, js):
+        def deal_scales(a):
             raw = ws_raw[:, :, a * SPAN : (a + 1) * SPAN]
             nc.vector.tensor_copy(
-                out=ws_dealt[a][:, js], in_=raw.rearrange("p g (m j) -> p j g m", j=PACK)[:, js]
+                out=ws_dealt[a][:], in_=raw.rearrange("p g (m j) -> p j g m", j=PACK)
             )
 
         def quantize(codes, scales, values):
@@ -114,16 +103,18 @@ def tile_mix_xres_fm_pl_res_kernel(
 
         acc = {}
 
-        def mm(a, j, g, tier):
+        def mm(a, j, g, tier, cols=WHOLE, bank=None):
             first = tier == "x4" and g == 0
             if first:
-                acc[a, j] = psum.tile([P, T], F32, name="bank%d" % ((a * PACK + j) % BANKS))
+                bank = (a * PACK + j) % BANKS if bank is None else bank
+                acc[a, j, cols.start] = psum.tile([P, T], F32, name="bank%d" % bank)
             if tier == "x4":
-                rhs, rhs_scale = x4_sb[:, g, :].bitcast(FP4X4), x4s_sb[:, g, :]
+                rhs = x4_sb[:, g, 2 * cols.start : 2 * cols.stop].bitcast(FP4X4)
+                rhs_scale = x4s_sb[:, g, cols]
             else:
-                rhs, rhs_scale = xr_codes[g][:].bitcast(FP8X4), xr_scales[g][:]
+                rhs, rhs_scale = xr_codes[g][:, cols].bitcast(FP8X4), xr_scales[g][:, cols]
             nc.tensor.matmul_mx(
-                out=acc[a, j][:],
+                out=acc[a, j, cols.start][:, cols],
                 lhsT=w_dealt[a][:, j, g, :].bitcast(FP4X4),
                 lhsT_scale=ws_dealt[a][:, j, g, :],
                 rhs=rhs,
@@ -132,10 +123,19 @@ def tile_mix_xres_fm_pl_res_kernel(
                 stop=(tier == "xr" and g == PASSES - 1),
             )
 
+        def group(a, j, cols=WHOLE, bank=None):
+            for tier in ("x4", "xr"):
+                for g in range(PASSES):
+                    mm(a, j, g, tier, cols, bank)
+
         def add(a, j, cols):
+            sums = acc.get((a, j, cols.start), acc[a, j, 0])
             nc.vector.tensor_tensor(
-                out=o_f32[a][:, j, cols], in0=acc[a, j][:, cols], in1=r_sb[a][:, j, cols], op=ADD
+                out=o_f32[a][:, j, cols], in0=sums[:, cols], in1=r_sb[a][:, j, cols], op=ADD
             )
+
+        def round_out(copy, a, cols):
+            interleave(copy, o_bf[a], o_f32[a], cols)
 
         def store_rows(a, js):
             nc.sync.dma_start(out=rows_of(out_0, a)[:, js], in_=o_f32[a][:, js])
@@ -146,10 +146,35 @@ def tile_mix_xres_fm_pl_res_kernel(
 
         codes_hbm = out_1.rearrange("a p t i -> p a (t i)").bitcast(I32)
 
-        def store_scales():
+        def store_early_codes():
+            nc.sync.dma_start(out=codes_hbm[:, :last], in_=codes_early[:].bitcast(I32))
+
+        def store_late_codes(cols):
+            nc.sync.dma_start(out=codes_hbm[:, last, cols], in_=codes_late[:, cols].bitcast(I32))
+
+        def store_scales(queues):
             rows = out_2.bitcast(I32).rearrange("a (q i) n -> i q a n", i=4)
-            for i in range(4):
-                nc.sync.dma_start(out=rows[i], in_=o_scales[OUT_PLANE_ROW + i : P : 32].bitcast(I32))
+            for i, queue in enumerate(queues):
+                queue.dma_start(out=rows[i], in_=o_scales[OUT_PLANE_ROW + i : P : 32].bitcast(I32))
+
+        vcopy, scopy = nc.vector.tensor_copy, nc.scalar.copy
+
+        nc.vector.memset(ws_raw[:].bitcast(I32), 0)
+        nc.vector.memset(x4s_sb[:].bitcast(I32), 0)
+
+        nc.sync.dma_start(
+            out=x4_sb[:].bitcast(I32), in_=x4_words.bitcast(I32).rearrange("g p n -> p g n")
+        )
+        load_scale_rows(ws_raw, w4_scales)
+        nc.sync.dma_start(out=w_early[:].bitcast(I32), in_=w_hbm[:, :, :early_words])
+        load_scale_rows(x4s_sb, x4_scales)
+        for g in range(PASSES):
+            nc.sync.dma_start(out=xr_f32[g][:], in_=rows_of(xr, g))
+        load_r(0, EVERY)
+        nc.sync.dma_start(out=w_late[:].bitcast(I32), in_=w_hbm[:, :, early_words:])
+        load_r(1, FRONT)
+        load_r(1, BACK)
+        load_r(last, EVERY)
 
         warm = psum.tile([P, T], F32, name="bank%d" % (BANKS - 1))
         for step in range(WARM_PASSES):
@@ -163,62 +188,69 @@ def tile_mix_xres_fm_pl_res_kernel(
                 stop=True,
             )
 
-        front, back, every = slice(0, 2), slice(2, PACK), slice(0, PACK)
-        deal_scales(0, every)
-        deal_words(0, front)
-        deal_words(0, back)
-        deal_scales(1, every)
-        deal_words(1, every)
-        deal_scales(2, every)
-        for a in range(2):
+        deal_scales(0)
+        deal_words(vcopy, 0, FRONT)
+        deal_words(vcopy, 0, BACK)
+        deal_scales(1)
+        deal_words(vcopy, 1, EVERY)
+        deal_scales(last)
+        for a in range(last):
             for j in range(PACK):
                 for g in range(PASSES):
                     mm(a, j, g, "x4")
 
         for g in range(PASSES):
             split = HALF + XR_SCALAR_COLS
-            interleave(nc.scalar.copy, xr_bf[g], xr_f32[g], slice(HALF, split))
-            interleave(nc.vector.tensor_copy, xr_bf[g], xr_f32[g], LEFT)
-            interleave(nc.vector.tensor_copy, xr_bf[g], xr_f32[g], slice(split, T))
+            interleave(scopy, xr_bf[g], xr_f32[g], slice(HALF, split))
+            interleave(vcopy, xr_bf[g], xr_f32[g], LEFT)
+            interleave(vcopy, xr_bf[g], xr_f32[g], slice(split, T))
             for cols in (LEFT, RIGHT):
                 quantize(xr_codes[g][:, cols], xr_scales[g][:, cols], xr_bf[g][:, cols, :])
 
-        deal_words(last, every)
         for j in range(PACK):
             mm(0, j, 0, "xr")
         for j in range(EARLY_GROUPS):
             mm(1, j, 0, "xr")
-        for a in range(2):
-            for j in range(PACK):
-                if a == 1 and j >= EARLY_GROUPS:
-                    mm(a, j, 0, "xr")
-                mm(a, j, 1, "xr")
-                add(a, j, LEFT)
-            interleave(nc.scalar.copy, o_bf[a], o_f32[a], LEFT)
-            for j in range(PACK):
-                add(a, j, RIGHT)
-                if j % 2:
-                    store_rows(a, slice(j - 1, j + 1))
-            interleave(nc.scalar.copy, o_bf[a], o_f32[a], RIGHT)
+        for j in range(PACK):
+            mm(0, j, 1, "xr")
+            add(0, j, LEFT)
+        deal_words(scopy, last, FRONT)
+        round_out(scopy, 0, LEFT)
+        for j in range(PACK):
+            add(0, j, RIGHT)
+        store_rows(0, EVERY)
+        round_out(scopy, 0, RIGHT)
+        deal_words(scopy, last, BACK)
+
+        for j in range(PACK):
+            if j >= EARLY_GROUPS:
+                mm(1, j, 0, "xr")
+            mm(1, j, 1, "xr")
+            add(1, j, WHOLE if j < 2 else LEFT)
+        round_out(scopy, 1, LEFT)
+        for j in range(2, PACK):
+            add(1, j, RIGHT)
+        store_rows(1, EVERY)
+        round_out(scopy, 1, RIGHT)
 
         quantize_out(0, WHOLE)
-        for j in range(PACK):
-            for tier in ("x4", "xr"):
-                for g in range(PASSES):
-                    mm(last, j, g, tier)
-            if j < PACK - 1:
-                add(last, j, WHOLE)
-            if j == 1:
-                store_rows(last, slice(0, 2))
+        for j in range(2):
+            group(last, j)
+            add(last, j, WHOLE)
+        store_rows(last, FRONT)
+        for j in range(2, PACK):
+            group(last, j, LEFT)
+            add(last, j, LEFT)
+        round_out(scopy, last, LEFT)
         quantize_out(1, WHOLE)
-        nc.sync.dma_start(out=codes_hbm[:, :last], in_=codes_early[:].bitcast(I32))
-        add(last, PACK - 1, LEFT)
-        interleave(nc.scalar.copy, o_bf[last], o_f32[last], slice(0, TAIL_SCALAR_COLS))
-        add(last, PACK - 1, RIGHT)
-        store_rows(last, slice(2, PACK))
-        interleave(nc.vector.tensor_copy, o_bf[last], o_f32[last], slice(TAIL_SCALAR_COLS, HALF))
-        interleave(nc.vector.tensor_copy, o_bf[last], o_f32[last], RIGHT)
+        store_early_codes()
+        for j in range(2, PACK):
+            group(last, j, RIGHT, j + 2)
+            add(last, j, RIGHT)
+        store_rows(last, BACK)
+        round_out(scopy, last, slice(HALF, T - TAIL_VECTOR_COLS))
+        round_out(vcopy, last, slice(T - TAIL_VECTOR_COLS, T))
         for cols in (LEFT, RIGHT):
             quantize_out(last, cols)
-            nc.sync.dma_start(out=codes_hbm[:, last, cols], in_=codes_late[:, cols].bitcast(I32))
-        store_scales()
+            store_late_codes(cols)
+        store_scales([nc.scalar, nc.scalar, nc.sync, nc.sync])

@@ -27,7 +27,7 @@ HALF = T // 2
 LEFT, RIGHT, WHOLE = slice(0, HALF), slice(HALF, T), slice(0, T)
 FRONT, BACK, EVERY = slice(0, 2), slice(2, PACK), slice(0, PACK)
 EARLY_GROUPS = 0
-TAIL_VECTOR_COLS = 128
+TAIL_SCALAR_COLS = 192
 XR_SCALAR_COLS = 176
 
 
@@ -234,23 +234,21 @@ def tile_mix_xres_fm_pl_res_kernel(
         round_out(scopy, 1, RIGHT)
 
         quantize_out(0, WHOLE)
-        for j in range(2):
+        for j in range(PACK - 1):
             group(last, j)
             add(last, j, WHOLE)
-        store_rows(last, FRONT)
-        for j in range(2, PACK):
-            group(last, j, LEFT)
-            add(last, j, LEFT)
-        round_out(scopy, last, LEFT)
+            if j == 1:
+                store_rows(last, FRONT)
         quantize_out(1, WHOLE)
         store_early_codes()
-        for j in range(2, PACK):
-            group(last, j, RIGHT, j + 2)
-            add(last, j, RIGHT)
+        group(last, PACK - 1)
+        add(last, PACK - 1, LEFT)
+        round_out(scopy, last, slice(0, TAIL_SCALAR_COLS))
+        add(last, PACK - 1, RIGHT)
         store_rows(last, BACK)
-        round_out(scopy, last, slice(HALF, T - TAIL_VECTOR_COLS))
-        round_out(vcopy, last, slice(T - TAIL_VECTOR_COLS, T))
+        round_out(vcopy, last, slice(TAIL_SCALAR_COLS, HALF))
+        round_out(vcopy, last, RIGHT)
         for cols in (LEFT, RIGHT):
             quantize_out(last, cols)
             store_late_codes(cols)
-        store_scales([nc.scalar, nc.scalar, nc.sync, nc.sync])
+        store_scales([nc.sync] * 4)

@@ -27,7 +27,7 @@ HALF = T // 2
 LEFT, RIGHT, WHOLE = slice(0, HALF), slice(HALF, T), slice(0, T)
 FRONT, BACK, EVERY = slice(0, 2), slice(2, PACK), slice(0, PACK)
 EARLY_GROUPS = 0
-TAIL_SCALAR_COLS = 192
+TAIL_FIRST, TAIL_LAST = 128, 416
 XR_SCALAR_COLS = 176
 
 
@@ -172,8 +172,7 @@ def tile_mix_xres_fm_pl_res_kernel(
             nc.sync.dma_start(out=xr_f32[g][:], in_=rows_of(xr, g))
         load_r(0, EVERY)
         nc.sync.dma_start(out=w_late[:].bitcast(I32), in_=w_hbm[:, :, early_words:])
-        load_r(1, FRONT)
-        load_r(1, BACK)
+        load_r(1, EVERY)
         load_r(last, EVERY)
 
         warm = psum.tile([P, T], F32, name="bank%d" % (BANKS - 1))
@@ -215,22 +214,23 @@ def tile_mix_xres_fm_pl_res_kernel(
             mm(0, j, 1, "xr")
             add(0, j, LEFT)
         deal_words(scopy, last, FRONT)
+        deal_words(scopy, last, BACK)
         round_out(scopy, 0, LEFT)
         for j in range(PACK):
             add(0, j, RIGHT)
         store_rows(0, EVERY)
         round_out(scopy, 0, RIGHT)
-        deal_words(scopy, last, BACK)
 
         for j in range(PACK):
             if j >= EARLY_GROUPS:
                 mm(1, j, 0, "xr")
             mm(1, j, 1, "xr")
-            add(1, j, WHOLE if j < 2 else LEFT)
+            add(1, j, LEFT)
         round_out(scopy, 1, LEFT)
-        for j in range(2, PACK):
+        for j in range(PACK):
             add(1, j, RIGHT)
-        store_rows(1, EVERY)
+            if j % 2:
+                store_rows(1, slice(j - 1, j + 1))
         round_out(scopy, 1, RIGHT)
 
         quantize_out(0, WHOLE)
@@ -243,11 +243,12 @@ def tile_mix_xres_fm_pl_res_kernel(
         store_early_codes()
         group(last, PACK - 1)
         add(last, PACK - 1, LEFT)
-        round_out(scopy, last, slice(0, TAIL_SCALAR_COLS))
+        round_out(scopy, last, slice(0, TAIL_FIRST))
         add(last, PACK - 1, RIGHT)
         store_rows(last, BACK)
-        round_out(vcopy, last, slice(TAIL_SCALAR_COLS, HALF))
-        round_out(vcopy, last, RIGHT)
+        round_out(scopy, last, slice(TAIL_LAST, T))
+        round_out(vcopy, last, slice(TAIL_FIRST, HALF))
+        round_out(vcopy, last, slice(HALF, TAIL_LAST))
         for cols in (LEFT, RIGHT):
             quantize_out(last, cols)
             store_late_codes(cols)

from contextlib import ExitStack

import concourse.mybir as mybir

K, M, T = 1024, 1536, 512
FLOPS = 2 * 2 * K * M * T

F32 = mybir.dt.float32
BF16 = mybir.dt.bfloat16
I32 = mybir.dt.int32
U32 = mybir.dt.uint32
U16 = mybir.dt.uint16
U8 = mybir.dt.uint8
FP8X4 = mybir.dt.float8_e4m3fn_x4
FP4X4 = mybir.dt.float4_e2m1fn_x4
ADD = mybir.AluOpType.add

P = 128
PACK = 4
SPAN = P * PACK
PASSES = K // SPAN
BLOCKS = M // SPAN
BANKS = 8
WARM_PASSES = 4
OUT_PLANE_ROW = 4
HALF = T // 2
LEFT, RIGHT, WHOLE = slice(0, HALF), slice(HALF, T), slice(0, T)
FRONT, BACK, EVERY = slice(0, 2), slice(2, PACK), slice(0, PACK)
EARLY_GROUPS = 0
TAIL_FIRST, TAIL_LAST = 128, 416
XR_SCALAR_COLS = 176


def interleave(copy, dst, src, cols):
    copy(
        out=dst[:, cols, :].rearrange("p (c i) j -> p c j i", i=PACK),
        in_=src[:, :, cols].rearrange("p j (c i) -> p c j i", i=PACK),
    )


def tile_mix_xres_fm_pl_res_kernel(
    tc, x4_words, x4_scales, xr, w4_words, w4_scales, r, out_0, out_1, out_2
):
    nc = tc.nc
    with ExitStack() as ctx:
        sb = ctx.enter_context(tc.tile_pool(name="sb", bufs=1))
        psum = ctx.enter_context(tc.psum_pool(name="psum", bufs=1))
        ctx.enter_context(tc.manual_schedule())

        def tile(name, shape, dtype):
            return sb.tile(shape, dtype, name=name, align_bytes=256)

        last = BLOCKS - 1
        w_early = tile("w_early", [P, PASSES, last * 2 * SPAN], U8)
        w_late = tile("w_late", [P, PASSES, 2 * SPAN], U8)
        ws_raw = tile("ws_raw", [P, PASSES, M], U8)
        w_dealt = [tile("w_dealt%d" % a, [P, PACK, PASSES, 2 * P], U8) for a in range(BLOCKS)]
        ws_dealt = [tile("ws_dealt%d" % a, [P, PACK, PASSES, P], U8) for a in range(BLOCKS)]
        x4_sb = tile("x4_sb", [P, PASSES, 2 * T], U8)
        x4s_sb = tile("x4s_sb", [P, PASSES, T], U8)
        xr_f32 = [tile("xr_f32_%d" % g, [P, PACK, T], F32) for g in range(PASSES)]
        xr_bf = [tile("xr_bf%d" % g, [P, T, PACK], BF16) for g in range(PASSES)]
        xr_codes = [tile("xr_codes%d" % g, [P, T], U32) for g in range(PASSES)]
        xr_scales = [tile("xr_scales%d" % g, [P, T], U8) for g in range(PASSES)]
        r_sb = [tile("r_sb%d" % a, [P, PACK, T], F32) for a in range(BLOCKS)]
        o_f32 = [tile("o_f32_%d" % a, [P, PACK, T], F32) for a in range(BLOCKS)]
        o_bf = [tile("o_bf%d" % a, [P, T, PACK], BF16) for a in range(BLOCKS)]
        codes_early = tile("codes_early", [P, last, T], U32)
        codes_late = tile("codes_late", [P, T], U32)
        o_scales = tile("o_scales", [P, BLOCKS, T], U8)

        w_hbm = w4_words.bitcast(I32).rearrange("g p n -> p g n")
        early_words = last * 2 * SPAN // 4

        def load_scale_rows(plane, scales):
            rows = scales.bitcast(I32).rearrange("g (q i) n -> i q g n", i=4)
            for i in range(4):
                nc.sync.dma_start(out=plane[i:P:32].bitcast(I32), in_=rows[i])

        def rows_of(hbm, a):
            return hbm[a * SPAN : (a + 1) * SPAN, :].rearrange("(p j) t -> p j t", j=PACK)

        def load_r(a, js):
            nc.sync.dma_start(out=r_sb[a][:, js], in_=rows_of(r, a)[:, js])

        def deal_words(copy, a, js):
            raw = w_late[:] if a == last else w_early[:, :, a * 2 * SPAN : (a + 1) * 2 * SPAN]
            copy(
                out=w_dealt[a][:, js].bitcast(U16),
                in_=raw.bitcast(U16).rearrange("p g (m j) -> p j g m", j=PACK)[:, js],
            )

        def deal_scales(a):
            raw = ws_raw[:, :, a * SPAN : (a + 1) * SPAN]
            nc.vector.tensor_copy(
                out=ws_dealt[a][:], in_=raw.rearrange("p g (m j) -> p j g m", j=PACK)
            )

        def quantize(codes, scales, values):
            nc.vector.quantize_mx(
                out=codes.bitcast(FP8X4), scales=scales, in_=values.rearrange("p t j -> p (t j)")
            )

        acc = {}

        def mm(a, j, g, tier, cols=WHOLE, bank=None):
            first = tier == "x4" and g == 0
            if first:
                bank = (a * PACK + j) % BANKS if bank is None else bank
                acc[a, j, cols.start] = psum.tile([P, T], F32, name="bank%d" % bank)
            if tier == "x4":
                rhs = x4_sb[:, g, 2 * cols.start : 2 * cols.stop].bitcast(FP4X4)
                rhs_scale = x4s_sb[:, g, cols]
            else:
                rhs, rhs_scale = xr_codes[g][:, cols].bitcast(FP8X4), xr_scales[g][:, cols]
            nc.tensor.matmul_mx(
                out=acc[a, j, cols.start][:, cols],
                lhsT=w_dealt[a][:, j, g, :].bitcast(FP4X4),
                lhsT_scale=ws_dealt[a][:, j, g, :],
                rhs=rhs,
                rhs_scale=rhs_scale,
                start=first,
                stop=(tier == "xr" and g == PASSES - 1),
            )

        def group(a, j, cols=WHOLE, bank=None):
            for tier in ("x4", "xr"):
                for g in range(PASSES):
                    mm(a, j, g, tier, cols, bank)

        def add(a, j, cols):
            sums = acc.get((a, j, cols.start), acc[a, j, 0])
            nc.vector.tensor_tensor(
                out=o_f32[a][:, j, cols], in0=sums[:, cols], in1=r_sb[a][:, j, cols], op=ADD
            )

        def round_out(copy, a, cols):
            interleave(copy, o_bf[a], o_f32[a], cols)

        def store_rows(a, js):
            nc.sync.dma_start(out=rows_of(out_0, a)[:, js], in_=o_f32[a][:, js])

        def quantize_out(a, cols):
            codes = codes_late[:, cols] if a == last else codes_early[:, a, cols]
            quantize(codes, o_scales[OUT_PLANE_ROW:P, a, cols], o_bf[a][:, cols, :])

        codes_hbm = out_1.rearrange("a p t i -> p a (t i)").bitcast(I32)

        def store_early_codes():
            nc.sync.dma_start(out=codes_hbm[:, :last], in_=codes_early[:].bitcast(I32))

        def store_late_codes(cols):
            nc.sync.dma_start(out=codes_hbm[:, last, cols], in_=codes_late[:, cols].bitcast(I32))

        def store_scales(queues):
            rows = out_2.bitcast(I32).rearrange("a (q i) n -> i q a n", i=4)
            for i, queue in enumerate(queues):
                queue.dma_start(out=rows[i], in_=o_scales[OUT_PLANE_ROW + i : P : 32].bitcast(I32))

        vcopy, scopy = nc.vector.tensor_copy, nc.scalar.copy

        nc.vector.memset(ws_raw[:].bitcast(I32), 0)
        nc.vector.memset(x4s_sb[:].bitcast(I32), 0)

        nc.sync.dma_start(
            out=x4_sb[:].bitcast(I32), in_=x4_words.bitcast(I32).rearrange("g p n -> p g n")
        )
        load_scale_rows(ws_raw, w4_scales)
        nc.sync.dma_start(out=w_early[:].bitcast(I32), in_=w_hbm[:, :, :early_words])
        load_scale_rows(x4s_sb, x4_scales)
        for g in range(PASSES):
            nc.sync.dma_start(out=xr_f32[g][:], in_=rows_of(xr, g))
        load_r(0, EVERY)
        nc.sync.dma_start(out=w_late[:].bitcast(I32), in_=w_hbm[:, :, early_words:])
        load_r(1, EVERY)
        load_r(last, EVERY)

        warm = psum.tile([P, T], F32, name="bank%d" % (BANKS - 1))
        for step in range(WARM_PASSES):
            nc.tensor.matmul_mx(
                out=warm[:],
                lhsT=x4_sb[:, 0, : 2 * P].bitcast(FP4X4),
                lhsT_scale=x4_sb[:, 1, :P],
                rhs=x4_sb[:, 0, :].bitcast(FP4X4),
                rhs_scale=x4_sb[:, 1, :T],
                start=True,
                stop=True,
            )

        deal_scales(0)
        deal_words(vcopy, 0, FRONT)
        deal_words(vcopy, 0, BACK)
        deal_scales(1)
        deal_words(vcopy, 1, EVERY)
        deal_scales(last)
        for a in range(last):
            for j in range(PACK):
                for g in range(PASSES):
                    mm(a, j, g, "x4")

        for g in range(PASSES):
            split = HALF + XR_SCALAR_COLS
            interleave(scopy, xr_bf[g], xr_f32[g], slice(HALF, split))
            interleave(vcopy, xr_bf[g], xr_f32[g], LEFT)
            interleave(vcopy, xr_bf[g], xr_f32[g], slice(split, T))
            for cols in (LEFT, RIGHT):
                quantize(xr_codes[g][:, cols], xr_scales[g][:, cols], xr_bf[g][:, cols, :])

        for j in range(PACK):
            mm(0, j, 0, "xr")
        for j in range(EARLY_GROUPS):
            mm(1, j, 0, "xr")
        for j in range(PACK):
            mm(0, j, 1, "xr")
            add(0, j, LEFT)
        deal_words(scopy, last, FRONT)
        deal_words(scopy, last, BACK)
        round_out(scopy, 0, LEFT)
        for j in range(PACK):
            add(0, j, RIGHT)
        store_rows(0, EVERY)
        round_out(scopy, 0, RIGHT)

        for j in range(PACK):
            if j >= EARLY_GROUPS:
                mm(1, j, 0, "xr")
            mm(1, j, 1, "xr")
            add(1, j, LEFT)
        round_out(scopy, 1, LEFT)
        for j in range(PACK):
            add(1, j, RIGHT)
            if j % 2:
                store_rows(1, slice(j - 1, j + 1))
        round_out(scopy, 1, RIGHT)

        quantize_out(0, WHOLE)
        for j in range(PACK - 1):
            group(last, j)
            add(last, j, WHOLE)
            if j == 1:
                store_rows(last, FRONT)
        quantize_out(1, WHOLE)
        store_early_codes()
        group(last, PACK - 1)
        add(last, PACK - 1, LEFT)
        round_out(scopy, last, slice(0, TAIL_FIRST))
        add(last, PACK - 1, RIGHT)
        store_rows(last, BACK)
        round_out(scopy, last, slice(TAIL_LAST, T))
        round_out(vcopy, last, slice(TAIL_FIRST, HALF))
        round_out(vcopy, last, slice(HALF, TAIL_LAST))
        for cols in (LEFT, RIGHT):
            quantize_out(last, cols)
            store_late_codes(cols)
        store_scales([nc.sync] * 4)
